import numpy as np
import ml_dtypes


def mxq(x, axis, fmt="e4m3"):
    dtype, down = {"e4m3": (ml_dtypes.float8_e4m3fn, 7), "e5m2": (ml_dtypes.float8_e5m2, 14)}[fmt]
    v = np.moveaxis(np.asarray(x, np.float32).astype(ml_dtypes.bfloat16).astype(np.float64), axis, -1)
    blocks = v.reshape(v.shape[:-1] + (-1, 32))
    amax = np.abs(blocks).max(-1, keepdims=True)
    byte = np.maximum(np.where(amax > 0, np.frexp(amax)[1] - 1 + 127, 0) - down, 1)
    scale = np.exp2(byte - 127.0)
    codes = (blocks / scale).astype(np.float32).astype(dtype).astype(np.float64)
    return np.moveaxis((codes * scale).reshape(v.shape), -1, axis)


WIDE = False


def mx_kscale(k):
    if not WIDE:
        return np.ones(k)
    levels = np.array([10, -10, 5, -5, 0])
    if k % 512:
        return np.exp2(np.random.permutation(np.resize(levels, k // 32))).repeat(32)
    a = np.empty((k // 512, 16))
    for p in range(k // 512):
        a[p, :8] = np.random.permutation(np.resize(levels, 8))
        for g in range(8):
            far = levels[np.abs(levels - a[p, g]) >= 10]
            a[p, g + 8] = far[np.random.randint(len(far))]
    return np.exp2(a.ravel()).repeat(32)


def f64(x):
    return np.asarray(x).astype(np.float64)


def striped(idx):
    return np.tile(idx.reshape(-1, 16).T, (8, 1)).astype(np.uint16)


def unstriped(offs):
    return offs[:16].T.reshape(-1).astype(np.int64)


def silu(v):
    return v / (1.0 + np.exp(-np.maximum(v, -700.0)))


K, T, E, C, N = 2560, 768, 12, 128, 128


def by_expert(wq, xq):
    return np.concatenate([wq[e].T @ xq[:, e * C:(e + 1) * C] for e in range(E)], axis=1)


def setup_inputs():
    n = np.random.standard_normal
    s = mx_kscale(K)[:, None]
    first = np.random.permutation(np.repeat(np.arange(E), T // E))
    second = (first + 1 + np.random.permutation(np.repeat(np.arange(E - 1), -(-T // (E - 1)))[:T])) % E
    while np.bincount(second, minlength=E).max() != T // E:
        load = np.bincount(second, minlength=E); hi, lo = int(load.argmax()), int(load.argmin())
        t = np.flatnonzero((second == hi) & (first != lo))[0]; second[t] = lo
    slot_token = np.empty(E * C, np.int64); pos = np.empty((2, T), np.int64); fill = np.zeros(E, np.int64)
    place = np.stack([np.random.permutation(C) for _ in range(E)])
    for r, deal in enumerate((first, second)):
        for t in np.random.permutation(T):
            e = deal[t]; j = e * C + place[e, fill[e]]; fill[e] += 1; slot_token[j] = t; pos[r, t] = j
    g = np.random.uniform(0.2, 0.8, T)
    return {
        "xT": (n((K, T)) * s).astype(np.float32),
        "w": (n((E, K, N)) / np.sqrt(K) / s[None]).astype(np.float32),
        "b": (0.3 * n((N, E))).astype(np.float32),
        "gate": np.stack([np.tile(g, (N, 1)), np.tile(1.0 - g, (N, 1))]).astype(np.float32),
        "offs": striped(slot_token),
        "pos1": striped(pos[0]),
        "pos2": striped(pos[1]),
    }


def reference(xT, w, b, gate, offs, pos1, pos2):
    idx = unstriped(offs)
    xq = mxq(f64(xT)[:, idx], 0, "e4m3")
    y = by_expert(mxq(f64(w), 1, "e4m3"), xq)
    y = silu(y + np.repeat(f64(b), C, axis=1))
    return f64(gate[0]) * y[:, unstriped(pos1)] + f64(gate[1]) * y[:, unstriped(pos2)]

@@ -1,0 +1,166 @@
+from contextlib import ExitStack
+
+import concourse.mybir as mybir
+
+K, T, E, C, N = 2560, 768, 12, 128, 128
+
+F32 = mybir.dt.float32
+BF16 = mybir.dt.bfloat16
+U32 = mybir.dt.uint32
+U16 = mybir.dt.uint16
+U8 = mybir.dt.uint8
+FP8X4 = mybir.dt.float8_e4m3fn_x4
+MULT = mybir.AluOpType.mult
+SILU = mybir.ActivationFunctionType.Silu
+
+P = 128
+PACK = 4
+K_PASS = P * PACK
+PASSES = K // K_PASS
+SLOTS = E * C
+GATHER = 512
+GROUPS = SLOTS // GATHER
+HALF = T // 2
+
+FLOPS = 2 * SLOTS * K * N
+
+X_SCALAR = 640
+W_SCALAR = [5, 4, 5, 4, 5, 4, 5, 4, 5, 4, 3, 2]
+ORDER = "x0 x1 w0 x2 w1 w2 x3 w3 w4 x4 w5 w6 w7 w8 w9 b w10 w11"
+
+
+def cols(ap):
+    return ap.rearrange("p (c i) t -> p c t i", i=4)
+
+
+def rows(ap):
+    return ap.rearrange("p t (c i) -> p c t i", i=4)
+
+
+def tile_routed_moe_kernel(tc, xT, w, b, gate, offs, pos1, pos2, out):
+    nc = tc.nc
+    with ExitStack() as ctx:
+        keep = ctx.enter_context(tc.tile_pool(name="keep", bufs=1))
+        stage = ctx.enter_context(tc.tile_pool(name="stage", bufs=1))
+        psum = ctx.enter_context(tc.psum_pool(name="psum", bufs=8))
+
+        offs_sb = keep.tile([P, SLOTS // 16], U16, name="offs_sb")
+        pos1_sb = keep.tile([P, T // 16], U16, name="pos1_sb")
+        pos2_sb = keep.tile([P, T // 16], U16, name="pos2_sb")
+        warm = keep.tile([P, 1], F32, name="warm")
+
+        x_codes = [keep.tile([P, T], U32, name=f"x_codes{a}", align_bytes=64) for a in range(PASSES)]
+        x_scales = [keep.tile([P, T], U8, name=f"x_scales{s}", align_bytes=64) for s in range(2)]
+        g_codes = keep.tile([P, PASSES, SLOTS], U32, name="g_codes", align_bytes=64)
+        g_scales = [keep.tile([P, SLOTS], U8, name=f"g_scales{s}", align_bytes=64) for s in range(2)]
+        w_codes = keep.tile([P, E, PASSES, N], U32, name="w_codes", align_bytes=64)
+        w_scales = keep.tile([P, E, PASSES, N], U8, name="w_scales", align_bytes=64)
+
+        for s in range(2):
+            nc.gpsimd.memset(x_scales[s][:], 0)
+        nc.vector.memset(warm[:], 0.0)
+        nc.scalar.activation(warm[:], warm[:], SILU)
+
+        x_view = xT.rearrange("(a p t) n -> a p t n", p=P, t=PACK)
+        w_view = w.rearrange("e (a p t) n -> e p a t n", p=P, t=PACK)
+
+        def gather(dst, src):
+            for g in range(GROUPS):
+                nc.vector.tensor_copy(
+                    dst[:, g * GATHER : (g + 1) * GATHER],
+                    src[:].indirect(offs_sb[:, g * GATHER // 16 : (g + 1) * GATHER // 16]),
+                )
+
+        def tokens(a):
+            raw = stage.tile([P, PACK, T], F32, name="x_raw", tag="x_raw", bufs=3)
+            grouped = stage.tile([P, T, PACK], BF16, name="x_grouped", tag="x_grouped", bufs=2, align_bytes=64)
+            if a == 0:
+                loads = [(0, 256), (256, 512), (512, T)]
+                shares = [(nc.vector.tensor_copy, 0, 256), (nc.scalar.copy, 256, 512), (nc.vector.tensor_copy, 512, T)]
+            else:
+                loads = [(0, T)]
+                shares = [(nc.scalar.copy, 0, X_SCALAR), (nc.vector.tensor_copy, X_SCALAR, T)]
+            for lo, hi in loads:
+                nc.sync.dma_start(raw[:, :, lo:hi], x_view[a][:, :, lo:hi])
+            if a == 0:
+                nc.sync.dma_start(offs_sb[:], offs)
+            for copy, lo, hi in shares:
+                copy(cols(grouped[:, lo:hi, :]), rows(raw[:, :, lo:hi]))
+            flat = grouped[:].rearrange("p n t -> p (n t)")
+            plane = 4 * (a % 4)
+            for lo, hi in ((0, 512), (512, T)):
+                nc.vector.quantize_mx(
+                    out=x_codes[a][:, lo:hi].bitcast(FP8X4),
+                    scales=x_scales[a // 4][plane:, lo:hi],
+                    in_=flat[:, PACK * lo : PACK * hi],
+                )
+            gather(g_codes[:, a, :], x_codes[a])
+            if a >= 3:
+                gather(g_scales[a - 3], x_scales[a - 3])
+
+        def weights(e):
+            last = e == E - 1
+            raw = stage.tile([P, PASSES, PACK, N], F32, name="w_raw", tag="w_raw", bufs=7)
+            grouped = stage.tile([P, PASSES, N, PACK], BF16, name="w_grouped", tag="w_grouped", bufs=5, align_bytes=64)
+            for lo, hi in ((0, 2), (2, 4), (4, 5)) if last else ((0, 5),):
+                nc.sync.dma_start(raw[:, lo:hi], w_view[e][:, lo:hi])
+            s = W_SCALAR[e]
+            shares = [(nc.scalar.copy, 0, s)]
+            if last:
+                shares.extend([(nc.vector.tensor_copy, 2, 4), (nc.vector.tensor_copy, 4, 5)])
+            elif s < PASSES:
+                shares.append((nc.vector.tensor_copy, s, PASSES))
+            for copy, lo, hi in shares:
+                copy(
+                    grouped[:, lo:hi].rearrange("p a (c i) t -> p a c t i", i=4),
+                    raw[:, lo:hi].rearrange("p a t (c i) -> p a c t i", i=4),
+                )
+            flat = grouped[:].rearrange("p a n t -> p (a n t)")
+            codes = w_codes[:, e].rearrange("p a n -> p (a n)")
+            scales = w_scales[:, e].rearrange("p a n -> p (a n)")
+            for lo, hi in ((0, 2), (2, 4), (4, 5)) if last else ((0, 4), (4, 5)):
+                nc.vector.quantize_mx(
+                    out=codes[:, N * lo : N * hi].bitcast(FP8X4),
+                    scales=scales[:, N * lo : N * hi],
+                    in_=flat[:, PACK * N * lo : PACK * N * hi],
+                )
+
+        for item in ORDER.split(" "):
+            if item == "b":
+                b_sb = stage.tile([P, E], F32, name="b_sb", tag="w_raw", bufs=7)
+                nc.sync.dma_start(b_sb[:], b)
+            elif item.startswith("x"):
+                tokens(int(item.replace("x", "")))
+            else:
+                weights(int(item.replace("w", "")))
+
+        gate_sb = stage.tile([P, 2, T], F32, name="gate_sb", tag="w_raw", bufs=7)
+        nc.sync.dma_start(gate_sb[:], gate.rearrange("g p n -> p g n"))
+        nc.sync.dma_start(pos1_sb[:], pos1)
+        nc.sync.dma_start(pos2_sb[:], pos2)
+
+        y = stage.tile([P, SLOTS], F32, name="y", tag="x_raw", bufs=3)
+        for e in range(E):
+            slots = slice(e * C, (e + 1) * C)
+            acc = psum.tile([N, C], F32, name="acc")
+            for a in range(PASSES):
+                nc.tensor.matmul_mx(
+                    out=acc[:],
+                    lhsT=w_codes[:, e, a, :].bitcast(FP8X4),
+                    lhsT_scale=w_scales[:, e, a, :],
+                    rhs=g_codes[:, a, slots].bitcast(FP8X4),
+                    rhs_scale=g_scales[a // 4][4 * (a % 4) :, slots],
+                    start=(a == 0),
+                    stop=(a == PASSES - 1),
+                )
+            nc.scalar.activation(y[:, slots], acc[:], SILU, bias=b_sb[:, e : e + 1])
+
+        first = stage.tile([P, T], F32, name="first", tag="x_raw", bufs=3)
+        second = stage.tile([P, T], F32, name="second", tag="x_raw", bufs=3)
+        halves = [(slice(h * HALF, (h + 1) * HALF), slice(h * HALF // 16, (h + 1) * HALF // 16)) for h in range(2)]
+        for cut, idx in halves:
+            nc.vector.tensor_tensor(first[:, cut], y[:].indirect(pos1_sb[:, idx]), gate_sb[:, 0, cut], MULT)
+            nc.vector.tensor_tensor(second[:, cut], y[:].indirect(pos2_sb[:, idx]), gate_sb[:, 1, cut], MULT)
+        for cut, idx in halves:
+            nc.vector.tensor_add(first[:, cut], first[:, cut], second[:, cut])
+            nc.sync.dma_start(out[:, cut], first[:, cut])

@@ -24,8 +24,8 @@ HALF = T // 2
 
 FLOPS = 2 * SLOTS * K * N
 
-X_SCALAR = 640
-W_SCALAR = [5, 4, 5, 4, 5, 4, 5, 4, 5, 4, 3, 2]
+X_SCALAR = [384, 512, 512, 768, 768]
+W_SCALAR = [5, 5, 5, 5, 5, 5, 5, 5, 5, 4, 3, 2]
 ORDER = "x0 x1 w0 x2 w1 w2 x3 w3 w4 x4 w5 w6 w7 w8 w9 b w10 w11"
 
 
@@ -74,14 +74,12 @@ def tile_routed_moe_kernel(tc, xT, w, b, gate, offs, pos1, pos2, out):
         def tokens(a):
             raw = stage.tile([P, PACK, T], F32, name="x_raw", tag="x_raw", bufs=3)
             grouped = stage.tile([P, T, PACK], BF16, name="x_grouped", tag="x_grouped", bufs=2, align_bytes=64)
-            if a == 0:
-                loads = [(0, 256), (256, 512), (512, T)]
-                shares = [(nc.vector.tensor_copy, 0, 256), (nc.scalar.copy, 256, 512), (nc.vector.tensor_copy, 512, T)]
+            cut = X_SCALAR[a]
+            if cut < T:
+                shares = [(nc.scalar.copy, 0, cut), (nc.vector.tensor_copy, cut, T)]
             else:
-                loads = [(0, T)]
-                shares = [(nc.scalar.copy, 0, X_SCALAR), (nc.vector.tensor_copy, X_SCALAR, T)]
-            for lo, hi in loads:
-                nc.sync.dma_start(raw[:, :, lo:hi], x_view[a][:, :, lo:hi])
+                shares = [(nc.scalar.copy, 0, 512), (nc.scalar.copy, 512, T)]
+            nc.sync.dma_start(raw[:], x_view[a])
             if a == 0:
                 nc.sync.dma_start(offs_sb[:], offs)
             for copy, lo, hi in shares:
@@ -157,7 +155,7 @@ def tile_routed_moe_kernel(tc, xT, w, b, gate, offs, pos1, pos2, out):
 
         first = stage.tile([P, T], F32, name="first", tag="x_raw", bufs=3)
         second = stage.tile([P, T], F32, name="second", tag="x_raw", bufs=3)
-        halves = [(slice(h * HALF, (h + 1) * HALF), slice(h * HALF // 16, (h + 1) * HALF // 16)) for h in range(2)]
+        halves = [(slice(lo, hi), slice(lo // 16, hi // 16)) for lo, hi in ((0, 512), (512, T))]
         for cut, idx in halves:
             nc.vector.tensor_tensor(first[:, cut], y[:].indirect(pos1_sb[:, idx]), gate_sb[:, 0, cut], MULT)
             nc.vector.tensor_tensor(second[:, cut], y[:].indirect(pos2_sb[:, idx]), gate_sb[:, 1, cut], MULT)

@@ -24,9 +24,9 @@ HALF = T // 2
 
 FLOPS = 2 * SLOTS * K * N
 
-X_SCALAR = [384, 512, 512, 768, 768]
-W_SCALAR = [5, 5, 5, 5, 5, 5, 5, 5, 5, 4, 3, 2]
-ORDER = "x0 x1 w0 x2 w1 w2 x3 w3 w4 x4 w5 w6 w7 w8 w9 b w10 w11"
+X_SCALAR = [256, 640, 768, 640, 640]
+W_SCALAR = [5, 5, 5, 5, 5, 4, 5, 5, 4, 3, 2, 2]
+ORDER = "x0 x1 x2 w0 x3 w1 w2 w3 x4 w4 w5 w6 w7 w8 w9 w10 b w11"
 
 
 def cols(ap):

@@ -24,9 +24,10 @@ HALF = T // 2
 
 FLOPS = 2 * SLOTS * K * N
 
-X_SCALAR = [256, 640, 768, 640, 640]
-W_SCALAR = [5, 5, 5, 5, 5, 4, 5, 5, 4, 3, 2, 2]
-ORDER = "x0 x1 x2 w0 x3 w1 w2 w3 x4 w4 w5 w6 w7 w8 w9 w10 b w11"
+X_SCALAR = [256, 768, 768, 640, 640]
+W_LOADS = [[(0, 5)]] * 10 + [[(0, 2), (2, 5)], [(0, 2), (2, 3), (3, 4), (4, 5)]]
+W_SCALAR = [5, 5, 5, 5, 5, 5, 5, 5, 4, 3, 2, 2]
+ORDER = "x0 x1 x2 w0 x3 w1 w2 x4 w3 w4 w5 w6 w7 w8 w9 w10 b w11"
 
 
 def cols(ap):
@@ -100,12 +101,12 @@ def tile_routed_moe_kernel(tc, xT, w, b, gate, offs, pos1, pos2, out):
             last = e == E - 1
             raw = stage.tile([P, PASSES, PACK, N], F32, name="w_raw", tag="w_raw", bufs=7)
             grouped = stage.tile([P, PASSES, N, PACK], BF16, name="w_grouped", tag="w_grouped", bufs=5, align_bytes=64)
-            for lo, hi in ((0, 2), (2, 4), (4, 5)) if last else ((0, 5),):
+            for lo, hi in W_LOADS[e]:
                 nc.sync.dma_start(raw[:, lo:hi], w_view[e][:, lo:hi])
             s = W_SCALAR[e]
             shares = [(nc.scalar.copy, 0, s)]
             if last:
-                shares.extend([(nc.vector.tensor_copy, 2, 4), (nc.vector.tensor_copy, 4, 5)])
+                shares.extend([(nc.vector.tensor_copy, a, a + 1) for a in range(2, PASSES)])
             elif s < PASSES:
                 shares.append((nc.vector.tensor_copy, s, PASSES))
             for copy, lo, hi in shares:
@@ -155,9 +156,9 @@ def tile_routed_moe_kernel(tc, xT, w, b, gate, offs, pos1, pos2, out):
 
         first = stage.tile([P, T], F32, name="first", tag="x_raw", bufs=3)
         second = stage.tile([P, T], F32, name="second", tag="x_raw", bufs=3)
-        halves = [(slice(lo, hi), slice(lo // 16, hi // 16)) for lo, hi in ((0, 512), (512, T))]
+        nc.vector.tensor_tensor(first[:], y[:].indirect(pos1_sb[:]), gate_sb[:, 0, :], MULT)
+        halves = [(slice(h * HALF, (h + 1) * HALF), slice(h * HALF // 16, (h + 1) * HALF // 16)) for h in range(2)]
         for cut, idx in halves:
-            nc.vector.tensor_tensor(first[:, cut], y[:].indirect(pos1_sb[:, idx]), gate_sb[:, 0, cut], MULT)
             nc.vector.tensor_tensor(second[:, cut], y[:].indirect(pos2_sb[:, idx]), gate_sb[:, 1, cut], MULT)
         for cut, idx in halves:
             nc.vector.tensor_add(first[:, cut], first[:, cut], second[:, cut])

from contextlib import ExitStack

import concourse.mybir as mybir

K, T, E, C, N = 2560, 768, 12, 128, 128

F32 = mybir.dt.float32
BF16 = mybir.dt.bfloat16
U32 = mybir.dt.uint32
U16 = mybir.dt.uint16
U8 = mybir.dt.uint8
FP8X4 = mybir.dt.float8_e4m3fn_x4
MULT = mybir.AluOpType.mult
SILU = mybir.ActivationFunctionType.Silu

P = 128
PACK = 4
K_PASS = P * PACK
PASSES = K // K_PASS
SLOTS = E * C
GATHER = 512
GROUPS = SLOTS // GATHER
HALF = T // 2

FLOPS = 2 * SLOTS * K * N

X_SCALAR = [256, 768, 768, 640, 640]
W_LOADS = [[(0, 5)]] * 10 + [[(0, 2), (2, 5)], [(0, 2), (2, 3), (3, 4), (4, 5)]]
W_SCALAR = [5, 5, 5, 5, 5, 5, 5, 5, 4, 3, 2, 2]
ORDER = "x0 x1 x2 w0 x3 w1 w2 x4 w3 w4 w5 w6 w7 w8 w9 w10 b w11"


def cols(ap):
    return ap.rearrange("p (c i) t -> p c t i", i=4)


def rows(ap):
    return ap.rearrange("p t (c i) -> p c t i", i=4)


def tile_routed_moe_kernel(tc, xT, w, b, gate, offs, pos1, pos2, out):
    nc = tc.nc
    with ExitStack() as ctx:
        keep = ctx.enter_context(tc.tile_pool(name="keep", bufs=1))
        stage = ctx.enter_context(tc.tile_pool(name="stage", bufs=1))
        psum = ctx.enter_context(tc.psum_pool(name="psum", bufs=8))

        offs_sb = keep.tile([P, SLOTS // 16], U16, name="offs_sb")
        pos1_sb = keep.tile([P, T // 16], U16, name="pos1_sb")
        pos2_sb = keep.tile([P, T // 16], U16, name="pos2_sb")
        warm = keep.tile([P, 1], F32, name="warm")

        x_codes = [keep.tile([P, T], U32, name=f"x_codes{a}", align_bytes=64) for a in range(PASSES)]
        x_scales = [keep.tile([P, T], U8, name=f"x_scales{s}", align_bytes=64) for s in range(2)]
        g_codes = keep.tile([P, PASSES, SLOTS], U32, name="g_codes", align_bytes=64)
        g_scales = [keep.tile([P, SLOTS], U8, name=f"g_scales{s}", align_bytes=64) for s in range(2)]
        w_codes = keep.tile([P, E, PASSES, N], U32, name="w_codes", align_bytes=64)
        w_scales = keep.tile([P, E, PASSES, N], U8, name="w_scales", align_bytes=64)

        for s in range(2):
            nc.gpsimd.memset(x_scales[s][:], 0)
        nc.vector.memset(warm[:], 0.0)
        nc.scalar.activation(warm[:], warm[:], SILU)

        x_view = xT.rearrange("(a p t) n -> a p t n", p=P, t=PACK)
        w_view = w.rearrange("e (a p t) n -> e p a t n", p=P, t=PACK)

        def gather(dst, src):
            for g in range(GROUPS):
                nc.vector.tensor_copy(
                    dst[:, g * GATHER : (g + 1) * GATHER],
                    src[:].indirect(offs_sb[:, g * GATHER // 16 : (g + 1) * GATHER // 16]),
                )

        def tokens(a):
            raw = stage.tile([P, PACK, T], F32, name="x_raw", tag="x_raw", bufs=3)
            grouped = stage.tile([P, T, PACK], BF16, name="x_grouped", tag="x_grouped", bufs=2, align_bytes=64)
            cut = X_SCALAR[a]
            if cut < T:
                shares = [(nc.scalar.copy, 0, cut), (nc.vector.tensor_copy, cut, T)]
            else:
                shares = [(nc.scalar.copy, 0, 512), (nc.scalar.copy, 512, T)]
            nc.sync.dma_start(raw[:], x_view[a])
            if a == 0:
                nc.sync.dma_start(offs_sb[:], offs)
            for copy, lo, hi in shares:
                copy(cols(grouped[:, lo:hi, :]), rows(raw[:, :, lo:hi]))
            flat = grouped[:].rearrange("p n t -> p (n t)")
            plane = 4 * (a % 4)
            for lo, hi in ((0, 512), (512, T)):
                nc.vector.quantize_mx(
                    out=x_codes[a][:, lo:hi].bitcast(FP8X4),
                    scales=x_scales[a // 4][plane:, lo:hi],
                    in_=flat[:, PACK * lo : PACK * hi],
                )
            gather(g_codes[:, a, :], x_codes[a])
            if a >= 3:
                gather(g_scales[a - 3], x_scales[a - 3])

        def weights(e):
            last = e == E - 1
            raw = stage.tile([P, PASSES, PACK, N], F32, name="w_raw", tag="w_raw", bufs=7)
            grouped = stage.tile([P, PASSES, N, PACK], BF16, name="w_grouped", tag="w_grouped", bufs=5, align_bytes=64)
            for lo, hi in W_LOADS[e]:
                nc.sync.dma_start(raw[:, lo:hi], w_view[e][:, lo:hi])
            s = W_SCALAR[e]
            shares = [(nc.scalar.copy, 0, s)]
            if last:
                shares.extend([(nc.vector.tensor_copy, a, a + 1) for a in range(2, PASSES)])
            elif s < PASSES:
                shares.append((nc.vector.tensor_copy, s, PASSES))
            for copy, lo, hi in shares:
                copy(
                    grouped[:, lo:hi].rearrange("p a (c i) t -> p a c t i", i=4),
                    raw[:, lo:hi].rearrange("p a t (c i) -> p a c t i", i=4),
                )
            flat = grouped[:].rearrange("p a n t -> p (a n t)")
            codes = w_codes[:, e].rearrange("p a n -> p (a n)")
            scales = w_scales[:, e].rearrange("p a n -> p (a n)")
            for lo, hi in ((0, 2), (2, 4), (4, 5)) if last else ((0, 4), (4, 5)):
                nc.vector.quantize_mx(
                    out=codes[:, N * lo : N * hi].bitcast(FP8X4),
                    scales=scales[:, N * lo : N * hi],
                    in_=flat[:, PACK * N * lo : PACK * N * hi],
                )

        for item in ORDER.split(" "):
            if item == "b":
                b_sb = stage.tile([P, E], F32, name="b_sb", tag="w_raw", bufs=7)
                nc.sync.dma_start(b_sb[:], b)
            elif item.startswith("x"):
                tokens(int(item.replace("x", "")))
            else:
                weights(int(item.replace("w", "")))

        gate_sb = stage.tile([P, 2, T], F32, name="gate_sb", tag="w_raw", bufs=7)
        nc.sync.dma_start(gate_sb[:], gate.rearrange("g p n -> p g n"))
        nc.sync.dma_start(pos1_sb[:], pos1)
        nc.sync.dma_start(pos2_sb[:], pos2)

        y = stage.tile([P, SLOTS], F32, name="y", tag="x_raw", bufs=3)
        for e in range(E):
            slots = slice(e * C, (e + 1) * C)
            acc = psum.tile([N, C], F32, name="acc")
            for a in range(PASSES):
                nc.tensor.matmul_mx(
                    out=acc[:],
                    lhsT=w_codes[:, e, a, :].bitcast(FP8X4),
                    lhsT_scale=w_scales[:, e, a, :],
                    rhs=g_codes[:, a, slots].bitcast(FP8X4),
                    rhs_scale=g_scales[a // 4][4 * (a % 4) :, slots],
                    start=(a == 0),
                    stop=(a == PASSES - 1),
                )
            nc.scalar.activation(y[:, slots], acc[:], SILU, bias=b_sb[:, e : e + 1])

        first = stage.tile([P, T], F32, name="first", tag="x_raw", bufs=3)
        second = stage.tile([P, T], F32, name="second", tag="x_raw", bufs=3)
        nc.vector.tensor_tensor(first[:], y[:].indirect(pos1_sb[:]), gate_sb[:, 0, :], MULT)
        halves = [(slice(h * HALF, (h + 1) * HALF), slice(h * HALF // 16, (h + 1) * HALF // 16)) for h in range(2)]
        for cut, idx in halves:
            nc.vector.tensor_tensor(second[:, cut], y[:].indirect(pos2_sb[:, idx]), gate_sb[:, 1, cut], MULT)
        for cut, idx in halves:
            nc.vector.tensor_add(first[:, cut], first[:, cut], second[:, cut])
            nc.sync.dma_start(out[:, cut], first[:, cut])
